import numpy as np
import ml_dtypes


def mxq(x, axis, fmt="e4m3"):
    dtype, down = {"e4m3": (ml_dtypes.float8_e4m3fn, 7), "e5m2": (ml_dtypes.float8_e5m2, 14)}[fmt]
    v = np.moveaxis(np.asarray(x, np.float32).astype(ml_dtypes.bfloat16).astype(np.float64), axis, -1)
    blocks = v.reshape(v.shape[:-1] + (-1, 32))
    amax = np.abs(blocks).max(-1, keepdims=True)
    byte = np.maximum(np.where(amax > 0, np.frexp(amax)[1] - 1 + 127, 0) - down, 1)
    scale = np.exp2(byte - 127.0)
    codes = (blocks / scale).astype(np.float32).astype(dtype).astype(np.float64)
    return np.moveaxis((codes * scale).reshape(v.shape), -1, axis)


WIDE = False


def mx_kscale(k):
    if not WIDE:
        return np.ones(k)
    levels = np.array([10, -10, 5, -5, 0])
    if k % 512:
        return np.exp2(np.random.permutation(np.resize(levels, k // 32))).repeat(32)
    a = np.empty((k // 512, 16))
    for p in range(k // 512):
        a[p, :8] = np.random.permutation(np.resize(levels, 8))
        for g in range(8):
            far = levels[np.abs(levels - a[p, g]) >= 10]
            a[p, g + 8] = far[np.random.randint(len(far))]
    return np.exp2(a.ravel()).repeat(32)


def f64(x):
    return np.asarray(x).astype(np.float64)


def striped(idx):
    return np.tile(idx.reshape(-1, 16).T, (8, 1)).astype(np.uint16)


def unstriped(offs):
    return offs[:16].T.reshape(-1).astype(np.int64)


def pack_weight(w):
    k, n = w.shape
    w = f64(np.asarray(w, np.float32).astype(ml_dtypes.bfloat16)).reshape(k // 32, 32, n)
    amax = np.abs(w).max(1)
    byte = np.clip(np.where(amax > 0, np.frexp(amax)[1] - 1 + 127 - 7, 1), 1, 254)
    scaled = (w * np.exp2(127.0 - byte)[:, None, :]).reshape(k, n).astype(np.float32)
    words = np.ascontiguousarray(scaled.reshape(k // 512, 128, 4, n).transpose(0, 1, 3, 2)).astype(ml_dtypes.float8_e4m3fn).view(np.uint8)
    return words, np.ascontiguousarray(byte.astype(np.uint8).reshape(k // 512, 16, n))


def unpack_weight(words, scales):
    g, p, n, _ = words.shape
    vals = np.ascontiguousarray(words).view(ml_dtypes.float8_e4m3fn).astype(np.float64) * np.repeat(np.exp2(scales.astype(np.float64) - 127.0), 8, axis=1)[..., None]
    return vals.transpose(0, 1, 3, 2).reshape(g * 512, n)


K, T, S, N, H, U = 1024, 1024, 512, 256, 512, 1024


def setup_inputs():
    n = np.random.standard_normal
    s = mx_kscale(K)[:, None]
    u = mx_kscale(H)
    packed_xT = pack_weight(n((K, T)) * s)
    return {
        "x_words": packed_xT[0],
        "x_scales": packed_xT[1],
        "w1": (n((K, H)) / np.sqrt(K) / s).astype(np.float32),
        "occ": (np.random.uniform(0.5, 2.0, (H, 1))).astype(np.float32),
        "unit": (np.random.uniform(0.6, 1.4, (H, 1)) * u[:, None]).astype(np.float32),
        "w2": (n((H, N)) / np.sqrt(H) / u[:, None]).astype(np.float32),
        "offs": striped(np.random.permutation(T)[:S]),
        "at1": striped(np.random.permutation(np.concatenate([np.arange(S), np.random.randint(0, S, U - S)]))),
        "at2": striped(np.random.permutation(np.concatenate([np.arange(S), np.random.randint(0, S, U - S)]))),
    }


def reference(x_words, x_scales, w1, occ, unit, w2, offs, at1, at2):
    xq = unpack_weight(x_words, x_scales)[:, unstriped(offs)]
    y = mxq(f64(w1), 0, "e4m3").T @ xq
    c1 = y[:, unstriped(at1)]
    c2 = y[:, unstriped(at2)]
    bo = f64(occ) * (c1 * c2)
    beta = np.exp(0.6 * np.tanh(bo))
    hid = f64(unit) * (bo * beta)
    return mxq(f64(w2), 0, "e4m3").T @ mxq(hid, 0, "e4m3")

@@ -1,0 +1,217 @@
+from contextlib import ExitStack
+
+import concourse.mybir as mybir
+
+F32 = mybir.dt.float32
+BF16 = mybir.dt.bfloat16
+I32 = mybir.dt.int32
+U32 = mybir.dt.uint32
+U16 = mybir.dt.uint16
+U8 = mybir.dt.uint8
+FP8X4 = mybir.dt.float8_e4m3fn_x4
+ALU = mybir.AluOpType
+ACT = mybir.ActivationFunctionType
+
+K, T, S, N, H, U = 1024, 1024, 512, 256, 512, 1024
+FLOPS = 2 * K * H * S + 2 * H * N * U
+
+P = 128
+PACK = 4
+K_PASS = P * PACK
+PASSES = K // K_PASS
+PER_COLUMN = 16
+BOND_CHUNKS = (256, 256, 256, 128, 128)
+W1_PIECES = (((0, 512),), ((0, 256), (256, 512)))
+SCALAR_EIGHTHS = 3
+
+
+def tile_picked_yhueck_sc_p_kernel(
+    tc, x_words, x_scales, w1, occ, unit, w2, offs, at1, at2, out
+):
+    nc = tc.nc
+    with ExitStack() as ctx:
+        held = ctx.enter_context(tc.tile_pool(name="held", bufs=1))
+        ring = ctx.enter_context(tc.tile_pool(name="ring", bufs=2))
+        psum_y = ctx.enter_context(tc.psum_pool(name="psum_y", bufs=1))
+        psum_out = ctx.enter_context(tc.psum_pool(name="psum_out", bufs=2))
+
+        offs_sb = held.tile([P, S // PER_COLUMN], U16, name="offs_sb")
+        nc.sync.dma_start(offs_sb[:], offs)
+
+        landed_bytes = held.tile([P, T], U8, name="landed_bytes", align_bytes=64)
+        x_bytes = held.tile([P, T], U8, name="x_bytes", align_bytes=64)
+        nc.vector.memset(x_bytes[:].bitcast(I32), 0)
+        for quad in range(4):
+            rows = slice(32 * quad, 32 * quad + 4 * PASSES)
+            nc.sync.dma_start(landed_bytes[rows, :].bitcast(I32), x_scales[:, 4 * quad : 4 * quad + 4, :].bitcast(I32))
+            nc.vector.tensor_copy(x_bytes[rows, :].bitcast(I32), landed_bytes[rows, :].bitcast(I32))
+
+        x_sb, w1_raw = {}, {}
+
+        def load_x(o):
+            x_sb[o] = held.tile([P, T], U32, name="x_sb%d" % o, align_bytes=64)
+            nc.sync.dma_start(x_sb[o][:].bitcast(I32), x_words[o].rearrange("p n t -> p (n t)").bitcast(I32))
+
+        def load_w1(o):
+            for c0, c1 in W1_PIECES[o]:
+                w1_raw[o, c0] = held.tile([P, PACK, c1 - c0], F32, name="w1_raw%d_%d" % (o, c0))
+                rows = w1[K_PASS * o : K_PASS * (o + 1), c0:c1]
+                nc.sync.dma_start(w1_raw[o, c0][:], rows.rearrange("(p j) c -> p j c", j=PACK))
+
+        load_x(0)
+        load_w1(0)
+        load_x(1)
+        occ_sb = held.tile([P, PACK], F32, name="occ_sb")
+        nc.sync.dma_start(occ_sb[:], occ.rearrange("(p t) o -> p (t o)", t=PACK))
+        unit_sb = held.tile([P, PACK], F32, name="unit_sb")
+        nc.sync.dma_start(unit_sb[:], unit.rearrange("(p t) o -> p (t o)", t=PACK))
+        at1_sb = held.tile([P, U // PER_COLUMN], U16, name="at1_sb")
+        nc.sync.dma_start(at1_sb[:], at1)
+        at2_sb = held.tile([P, U // PER_COLUMN], U16, name="at2_sb")
+        nc.sync.dma_start(at2_sb[:], at2)
+        load_w1(1)
+        w2_raw = held.tile([P, PACK, N], F32, name="w2_raw")
+        nc.sync.dma_start(w2_raw[:], w2.rearrange("(p j) n -> p j n", j=PACK))
+
+        def deal(o):
+            for c0, c1 in W1_PIECES[o]:
+                cut = (c1 - c0) * SCALAR_EIGHTHS // 8
+                for lo, hi in ((0, cut), (cut, c1 - c0)):
+                    dst = w1_grouped[o][:, :, (c0 + lo) // PACK : (c0 + hi) // PACK, :].rearrange("p t m j -> p m j t")
+                    src = w1_raw[o, c0][:, :, lo:hi].rearrange("p j (m t) -> p m j t", t=PACK)
+                    if lo == 0:
+                        nc.scalar.activation(dst, src, ACT.Copy)
+                    else:
+                        nc.vector.tensor_copy(dst, src)
+
+        picked_bytes = held.tile([P, S], U8, name="picked_bytes", align_bytes=64)
+        nc.vector.tensor_copy(picked_bytes[:], x_bytes[:].indirect(offs_sb[:]))
+
+        w1_grouped = {}
+        w1_codes = [held.tile([P, H], U32, name="w1_codes%d" % o, align_bytes=64) for o in range(PASSES)]
+        w1_planes = [held.tile([P, H], U8, name="w1_planes%d" % o, align_bytes=64) for o in range(PASSES)]
+        picked = {}
+
+        banks = [psum_y.tile([P, S], F32, name="y_bank%d" % t) for t in range(PACK)]
+
+        def first_product(o):
+            picked[o] = held.tile([P, S], U32, name="picked%d" % o, tag="turn%d" % o, align_bytes=64)
+            w1_grouped[o] = held.tile([P, PACK, P, PACK], BF16, name="w1_grouped%d" % o, tag="turn%d" % (o + 1), align_bytes=64)
+            nc.vector.tensor_copy(picked[o][:], x_sb[o][:].indirect(offs_sb[:]))
+            deal(o)
+            for t in range(PACK):
+                cols = slice(P * t, P * (t + 1))
+                nc.vector.quantize_mx(
+                    out=w1_codes[o][:, cols].bitcast(FP8X4),
+                    scales=w1_planes[o][:, cols],
+                    in_=w1_grouped[o][:, t, :, :].rearrange("p m j -> p (m j)"),
+                )
+                nc.tensor.matmul_mx(
+                    out=banks[t][:],
+                    lhsT=w1_codes[o][:, cols].bitcast(FP8X4),
+                    lhsT_scale=w1_planes[o][:, cols],
+                    rhs=picked[o][:].bitcast(FP8X4),
+                    rhs_scale=picked_bytes[4 * o : P, :],
+                    start=(o == 0),
+                    stop=(o == PASSES - 1),
+                )
+
+        for o in range(PASSES):
+            first_product(o)
+
+        weight = held.tile([P, PACK], F32, name="weight")
+        nc.vector.tensor_tensor(weight[:], occ_sb[:], unit_sb[:], ALU.mult)
+        unit_safe = held.tile([P, PACK], F32, name="unit_safe")
+        nc.vector.scalar_tensor_tensor(unit_safe[:], unit_sb[:], 0.0, unit_sb[:], ALU.is_equal, ALU.add)
+        unit_inv = held.tile([P, PACK], F32, name="unit_inv")
+        nc.vector.reciprocal(unit_inv[:], unit_safe[:])
+
+        y = [held.tile([P, S], F32, name="y%d" % t) for t in range(PACK)]
+        z = [held.tile([P, S], F32, name="z%d" % t) for t in range(PACK)]
+        nc.scalar.copy(y[0][:], banks[0][:])
+        for t in range(PACK):
+            if t + 1 < PACK:
+                nc.vector.tensor_copy(y[t + 1][:], banks[t + 1][:])
+            nc.vector.tensor_scalar(z[t][:], y[t][:], weight[:, t : t + 1], None, ALU.mult)
+
+        w2_grouped = held.tile([P, N, PACK], BF16, name="w2_grouped", align_bytes=64)
+        w2_codes = held.tile([P, N], U32, name="w2_codes", align_bytes=64)
+        w2_plane = held.tile([P, N], U8, name="w2_plane", align_bytes=64)
+
+        def quantise_w2():
+            nc.vector.tensor_copy(
+                w2_grouped[:].rearrange("p (c i) j -> p c j i", i=4),
+                w2_raw[:].rearrange("p j (c i) -> p c j i", i=4),
+            )
+            nc.vector.quantize_mx(
+                out=w2_codes[:].bitcast(FP8X4), scales=w2_plane[:], in_=w2_grouped[:].rearrange("p n j -> p (n j)")
+            )
+
+        starts = [sum(BOND_CHUNKS[:c]) for c in range(len(BOND_CHUNKS))]
+        orders, betas, sums = {}, {}, {}
+
+        def look_up(c):
+            n = BOND_CHUNKS[c]
+            entries = slice(starts[c] // PER_COLUMN, (starts[c] + n) // PER_COLUMN)
+            first = ring.tile([P, PACK, n], F32, name="first")
+            order = ring.tile([P, PACK, n], F32, name="order", bufs=3)
+            for t in range(PACK):
+                nc.scalar.activation(first[:, t, :], y[t][:].indirect(at1_sb[:, entries]), ACT.Copy)
+                nc.vector.tensor_tensor(order[:, t, :], z[t][:].indirect(at2_sb[:, entries]), first[:, t, :], ALU.mult)
+            orders[c] = order
+
+        def bend(c):
+            n = BOND_CHUNKS[c]
+            bent = ring.tile([P, PACK, n], F32, name="bent")
+            beta = ring.tile([P, PACK, n], F32, name="beta")
+            for t in range(PACK):
+                nc.scalar.activation(bent[:, t, :], orders[c][:, t, :], ACT.Tanh, scale=unit_inv[:, t : t + 1])
+            nc.scalar.activation(beta[:], bent[:], ACT.Exp, scale=0.6)
+            betas[c] = beta
+
+        def second_product(c):
+            n = BOND_CHUNKS[c]
+            hid = ring.tile([P, n, PACK], BF16, name="hid", align_bytes=64)
+            nc.vector.tensor_tensor(
+                hid[:].rearrange("p (g i) t -> p g t i", i=4),
+                orders[c][:].rearrange("p t (g i) -> p g t i", i=4),
+                betas[c][:].rearrange("p t (g i) -> p g t i", i=4),
+                ALU.mult,
+            )
+            hid_codes = ring.tile([P, n], U32, name="hid_codes", align_bytes=64)
+            hid_plane = ring.tile([P, n], U8, name="hid_plane", align_bytes=64)
+            nc.vector.quantize_mx(
+                out=hid_codes[:].bitcast(FP8X4), scales=hid_plane[:], in_=hid[:].rearrange("p n t -> p (n t)")
+            )
+            acc = [psum_out.tile([P, n], F32, name="acc%d" % a) for a in range(N // P)]
+            for a in range(N // P):
+                cols = slice(P * a, P * (a + 1))
+                nc.tensor.matmul_mx(
+                    out=acc[a][:],
+                    lhsT=w2_codes[:, cols].bitcast(FP8X4),
+                    lhsT_scale=w2_plane[:, cols],
+                    rhs=hid_codes[:].bitcast(FP8X4),
+                    rhs_scale=hid_plane[:],
+                    start=True,
+                    stop=True,
+                )
+            sums[c] = acc
+
+        def store(c):
+            n = BOND_CHUNKS[c]
+            result = ring.tile([P, N // P, n], F32, name="result", bufs=3)
+            nc.scalar.copy(result[:, 0, :], sums[c][0][:])
+            nc.vector.tensor_copy(result[:, 1, :], sums[c][1][:])
+            nc.sync.dma_start(out[:, starts[c] : starts[c] + n].rearrange("(a p) n -> p a n", p=P), result[:])
+
+        chunks = len(BOND_CHUNKS)
+        for step in range(chunks + 2):
+            if step < chunks:
+                look_up(step)
+            if step == 0:
+                quantise_w2()
+            if 0 <= step - 1 < chunks:
+                bend(step - 1)
+                second_product(step - 1)
+            if 0 <= step - 2 < chunks:
+                store(step - 2)

@@ -21,8 +21,7 @@ K_PASS = P * PACK
 PASSES = K // K_PASS
 PER_COLUMN = 16
 BOND_CHUNKS = (256, 256, 256, 128, 128)
-W1_PIECES = (((0, 512),), ((0, 256), (256, 512)))
-SCALAR_EIGHTHS = 3
+W1_PIECES = (((0, 512, 256),), ((0, 256, 256), (256, 512, 96)))
 
 
 def tile_picked_yhueck_sc_p_kernel(
@@ -53,7 +52,7 @@ def tile_picked_yhueck_sc_p_kernel(
             nc.sync.dma_start(x_sb[o][:].bitcast(I32), x_words[o].rearrange("p n t -> p (n t)").bitcast(I32))
 
         def load_w1(o):
-            for c0, c1 in W1_PIECES[o]:
+            for c0, c1, share in W1_PIECES[o]:
                 w1_raw[o, c0] = held.tile([P, PACK, c1 - c0], F32, name="w1_raw%d_%d" % (o, c0))
                 rows = w1[K_PASS * o : K_PASS * (o + 1), c0:c1]
                 nc.sync.dma_start(w1_raw[o, c0][:], rows.rearrange("(p j) c -> p j c", j=PACK))
@@ -74,9 +73,10 @@ def tile_picked_yhueck_sc_p_kernel(
         nc.sync.dma_start(w2_raw[:], w2.rearrange("(p j) n -> p j n", j=PACK))
 
         def deal(o):
-            for c0, c1 in W1_PIECES[o]:
-                cut = (c1 - c0) * SCALAR_EIGHTHS // 8
-                for lo, hi in ((0, cut), (cut, c1 - c0)):
+            for c0, c1, share in W1_PIECES[o]:
+                for lo, hi in ((0, share), (share, c1 - c0)):
+                    if lo == hi:
+                        continue
                     dst = w1_grouped[o][:, :, (c0 + lo) // PACK : (c0 + hi) // PACK, :].rearrange("p t m j -> p m j t")
                     src = w1_raw[o, c0][:, :, lo:hi].rearrange("p j (m t) -> p m j t", t=PACK)
                     if lo == 0:
@@ -156,7 +156,10 @@ def tile_picked_yhueck_sc_p_kernel(
             first = ring.tile([P, PACK, n], F32, name="first")
             order = ring.tile([P, PACK, n], F32, name="order", bufs=3)
             for t in range(PACK):
-                nc.scalar.activation(first[:, t, :], y[t][:].indirect(at1_sb[:, entries]), ACT.Copy)
+                if False:
+                    nc.vector.tensor_copy(first[:, t, :], y[t][:].indirect(at1_sb[:, entries]))
+                else:
+                    nc.scalar.activation(first[:, t, :], y[t][:].indirect(at1_sb[:, entries]), ACT.Copy)
                 nc.vector.tensor_tensor(order[:, t, :], z[t][:].indirect(at2_sb[:, entries]), first[:, t, :], ALU.mult)
             orders[c] = order
 
@@ -200,7 +203,10 @@ def tile_picked_yhueck_sc_p_kernel(
         def store(c):
             n = BOND_CHUNKS[c]
             result = ring.tile([P, N // P, n], F32, name="result", bufs=3)
-            nc.scalar.copy(result[:, 0, :], sums[c][0][:])
+            if c >= 3:
+                nc.scalar.copy(result[:, 0, :], sums[c][0][:])
+            else:
+                nc.vector.tensor_copy(result[:, 0, :], sums[c][0][:])
             nc.vector.tensor_copy(result[:, 1, :], sums[c][1][:])
             nc.sync.dma_start(out[:, starts[c] : starts[c] + n].rearrange("(a p) n -> p a n", p=P), result[:])
 

from contextlib import ExitStack

import concourse.mybir as mybir

F32 = mybir.dt.float32
BF16 = mybir.dt.bfloat16
I32 = mybir.dt.int32
U32 = mybir.dt.uint32
U16 = mybir.dt.uint16
U8 = mybir.dt.uint8
FP8X4 = mybir.dt.float8_e4m3fn_x4
ALU = mybir.AluOpType
ACT = mybir.ActivationFunctionType

K, T, S, N, H, U = 1024, 1024, 512, 256, 512, 1024
FLOPS = 2 * K * H * S + 2 * H * N * U

P = 128
PACK = 4
K_PASS = P * PACK
PASSES = K // K_PASS
PER_COLUMN = 16
BOND_CHUNKS = (256, 256, 256, 128, 128)
W1_PIECES = (((0, 512, 256),), ((0, 256, 256), (256, 512, 96)))


def tile_picked_yhueck_sc_p_kernel(
    tc, x_words, x_scales, w1, occ, unit, w2, offs, at1, at2, out
):
    nc = tc.nc
    with ExitStack() as ctx:
        held = ctx.enter_context(tc.tile_pool(name="held", bufs=1))
        ring = ctx.enter_context(tc.tile_pool(name="ring", bufs=2))
        psum_y = ctx.enter_context(tc.psum_pool(name="psum_y", bufs=1))
        psum_out = ctx.enter_context(tc.psum_pool(name="psum_out", bufs=2))

        offs_sb = held.tile([P, S // PER_COLUMN], U16, name="offs_sb")
        nc.sync.dma_start(offs_sb[:], offs)

        landed_bytes = held.tile([P, T], U8, name="landed_bytes", align_bytes=64)
        x_bytes = held.tile([P, T], U8, name="x_bytes", align_bytes=64)
        nc.vector.memset(x_bytes[:].bitcast(I32), 0)
        for quad in range(4):
            rows = slice(32 * quad, 32 * quad + 4 * PASSES)
            nc.sync.dma_start(landed_bytes[rows, :].bitcast(I32), x_scales[:, 4 * quad : 4 * quad + 4, :].bitcast(I32))
            nc.vector.tensor_copy(x_bytes[rows, :].bitcast(I32), landed_bytes[rows, :].bitcast(I32))

        x_sb, w1_raw = {}, {}

        def load_x(o):
            x_sb[o] = held.tile([P, T], U32, name="x_sb%d" % o, align_bytes=64)
            nc.sync.dma_start(x_sb[o][:].bitcast(I32), x_words[o].rearrange("p n t -> p (n t)").bitcast(I32))

        def load_w1(o):
            for c0, c1, share in W1_PIECES[o]:
                w1_raw[o, c0] = held.tile([P, PACK, c1 - c0], F32, name="w1_raw%d_%d" % (o, c0))
                rows = w1[K_PASS * o : K_PASS * (o + 1), c0:c1]
                nc.sync.dma_start(w1_raw[o, c0][:], rows.rearrange("(p j) c -> p j c", j=PACK))

        load_x(0)
        load_w1(0)
        load_x(1)
        occ_sb = held.tile([P, PACK], F32, name="occ_sb")
        nc.sync.dma_start(occ_sb[:], occ.rearrange("(p t) o -> p (t o)", t=PACK))
        unit_sb = held.tile([P, PACK], F32, name="unit_sb")
        nc.sync.dma_start(unit_sb[:], unit.rearrange("(p t) o -> p (t o)", t=PACK))
        at1_sb = held.tile([P, U // PER_COLUMN], U16, name="at1_sb")
        nc.sync.dma_start(at1_sb[:], at1)
        at2_sb = held.tile([P, U // PER_COLUMN], U16, name="at2_sb")
        nc.sync.dma_start(at2_sb[:], at2)
        load_w1(1)
        w2_raw = held.tile([P, PACK, N], F32, name="w2_raw")
        nc.sync.dma_start(w2_raw[:], w2.rearrange("(p j) n -> p j n", j=PACK))

        def deal(o):
            for c0, c1, share in W1_PIECES[o]:
                for lo, hi in ((0, share), (share, c1 - c0)):
                    if lo == hi:
                        continue
                    dst = w1_grouped[o][:, :, (c0 + lo) // PACK : (c0 + hi) // PACK, :].rearrange("p t m j -> p m j t")
                    src = w1_raw[o, c0][:, :, lo:hi].rearrange("p j (m t) -> p m j t", t=PACK)
                    if lo == 0:
                        nc.scalar.activation(dst, src, ACT.Copy)
                    else:
                        nc.vector.tensor_copy(dst, src)

        picked_bytes = held.tile([P, S], U8, name="picked_bytes", align_bytes=64)
        nc.vector.tensor_copy(picked_bytes[:], x_bytes[:].indirect(offs_sb[:]))

        w1_grouped = {}
        w1_codes = [held.tile([P, H], U32, name="w1_codes%d" % o, align_bytes=64) for o in range(PASSES)]
        w1_planes = [held.tile([P, H], U8, name="w1_planes%d" % o, align_bytes=64) for o in range(PASSES)]
        picked = {}

        banks = [psum_y.tile([P, S], F32, name="y_bank%d" % t) for t in range(PACK)]

        def first_product(o):
            picked[o] = held.tile([P, S], U32, name="picked%d" % o, tag="turn%d" % o, align_bytes=64)
            w1_grouped[o] = held.tile([P, PACK, P, PACK], BF16, name="w1_grouped%d" % o, tag="turn%d" % (o + 1), align_bytes=64)
            nc.vector.tensor_copy(picked[o][:], x_sb[o][:].indirect(offs_sb[:]))
            deal(o)
            for t in range(PACK):
                cols = slice(P * t, P * (t + 1))
                nc.vector.quantize_mx(
                    out=w1_codes[o][:, cols].bitcast(FP8X4),
                    scales=w1_planes[o][:, cols],
                    in_=w1_grouped[o][:, t, :, :].rearrange("p m j -> p (m j)"),
                )
                nc.tensor.matmul_mx(
                    out=banks[t][:],
                    lhsT=w1_codes[o][:, cols].bitcast(FP8X4),
                    lhsT_scale=w1_planes[o][:, cols],
                    rhs=picked[o][:].bitcast(FP8X4),
                    rhs_scale=picked_bytes[4 * o : P, :],
                    start=(o == 0),
                    stop=(o == PASSES - 1),
                )

        for o in range(PASSES):
            first_product(o)

        weight = held.tile([P, PACK], F32, name="weight")
        nc.vector.tensor_tensor(weight[:], occ_sb[:], unit_sb[:], ALU.mult)
        unit_safe = held.tile([P, PACK], F32, name="unit_safe")
        nc.vector.scalar_tensor_tensor(unit_safe[:], unit_sb[:], 0.0, unit_sb[:], ALU.is_equal, ALU.add)
        unit_inv = held.tile([P, PACK], F32, name="unit_inv")
        nc.vector.reciprocal(unit_inv[:], unit_safe[:])

        y = [held.tile([P, S], F32, name="y%d" % t) for t in range(PACK)]
        z = [held.tile([P, S], F32, name="z%d" % t) for t in range(PACK)]
        nc.scalar.copy(y[0][:], banks[0][:])
        for t in range(PACK):
            if t + 1 < PACK:
                nc.vector.tensor_copy(y[t + 1][:], banks[t + 1][:])
            nc.vector.tensor_scalar(z[t][:], y[t][:], weight[:, t : t + 1], None, ALU.mult)

        w2_grouped = held.tile([P, N, PACK], BF16, name="w2_grouped", align_bytes=64)
        w2_codes = held.tile([P, N], U32, name="w2_codes", align_bytes=64)
        w2_plane = held.tile([P, N], U8, name="w2_plane", align_bytes=64)

        def quantise_w2():
            nc.vector.tensor_copy(
                w2_grouped[:].rearrange("p (c i) j -> p c j i", i=4),
                w2_raw[:].rearrange("p j (c i) -> p c j i", i=4),
            )
            nc.vector.quantize_mx(
                out=w2_codes[:].bitcast(FP8X4), scales=w2_plane[:], in_=w2_grouped[:].rearrange("p n j -> p (n j)")
            )

        starts = [sum(BOND_CHUNKS[:c]) for c in range(len(BOND_CHUNKS))]
        orders, betas, sums = {}, {}, {}

        def look_up(c):
            n = BOND_CHUNKS[c]
            entries = slice(starts[c] // PER_COLUMN, (starts[c] + n) // PER_COLUMN)
            first = ring.tile([P, PACK, n], F32, name="first")
            order = ring.tile([P, PACK, n], F32, name="order", bufs=3)
            for t in range(PACK):
                if False:
                    nc.vector.tensor_copy(first[:, t, :], y[t][:].indirect(at1_sb[:, entries]))
                else:
                    nc.scalar.activation(first[:, t, :], y[t][:].indirect(at1_sb[:, entries]), ACT.Copy)
                nc.vector.tensor_tensor(order[:, t, :], z[t][:].indirect(at2_sb[:, entries]), first[:, t, :], ALU.mult)
            orders[c] = order

        def bend(c):
            n = BOND_CHUNKS[c]
            bent = ring.tile([P, PACK, n], F32, name="bent")
            beta = ring.tile([P, PACK, n], F32, name="beta")
            for t in range(PACK):
                nc.scalar.activation(bent[:, t, :], orders[c][:, t, :], ACT.Tanh, scale=unit_inv[:, t : t + 1])
            nc.scalar.activation(beta[:], bent[:], ACT.Exp, scale=0.6)
            betas[c] = beta

        def second_product(c):
            n = BOND_CHUNKS[c]
            hid = ring.tile([P, n, PACK], BF16, name="hid", align_bytes=64)
            nc.vector.tensor_tensor(
                hid[:].rearrange("p (g i) t -> p g t i", i=4),
                orders[c][:].rearrange("p t (g i) -> p g t i", i=4),
                betas[c][:].rearrange("p t (g i) -> p g t i", i=4),
                ALU.mult,
            )
            hid_codes = ring.tile([P, n], U32, name="hid_codes", align_bytes=64)
            hid_plane = ring.tile([P, n], U8, name="hid_plane", align_bytes=64)
            nc.vector.quantize_mx(
                out=hid_codes[:].bitcast(FP8X4), scales=hid_plane[:], in_=hid[:].rearrange("p n t -> p (n t)")
            )
            acc = [psum_out.tile([P, n], F32, name="acc%d" % a) for a in range(N // P)]
            for a in range(N // P):
                cols = slice(P * a, P * (a + 1))
                nc.tensor.matmul_mx(
                    out=acc[a][:],
                    lhsT=w2_codes[:, cols].bitcast(FP8X4),
                    lhsT_scale=w2_plane[:, cols],
                    rhs=hid_codes[:].bitcast(FP8X4),
                    rhs_scale=hid_plane[:],
                    start=True,
                    stop=True,
                )
            sums[c] = acc

        def store(c):
            n = BOND_CHUNKS[c]
            result = ring.tile([P, N // P, n], F32, name="result", bufs=3)
            if c >= 3:
                nc.scalar.copy(result[:, 0, :], sums[c][0][:])
            else:
                nc.vector.tensor_copy(result[:, 0, :], sums[c][0][:])
            nc.vector.tensor_copy(result[:, 1, :], sums[c][1][:])
            nc.sync.dma_start(out[:, starts[c] : starts[c] + n].rearrange("(a p) n -> p a n", p=P), result[:])

        chunks = len(BOND_CHUNKS)
        for step in range(chunks + 2):
            if step < chunks:
                look_up(step)
            if step == 0:
                quantise_w2()
            if 0 <= step - 1 < chunks:
                bend(step - 1)
                second_product(step - 1)
            if 0 <= step - 2 < chunks:
                store(step - 2)
